import numpy as np
import ml_dtypes

BF16 = ml_dtypes.bfloat16


def bf(x):
    return np.asarray(x, np.float32).astype(BF16)


def f32(x):
    return np.asarray(x, np.float32)


def f64(x):
    return np.asarray(x).astype(np.float64)


def striped(idx):
    return np.tile(idx.reshape(-1, 16).T, (8, 1))


S, K, M, N, E, Q = 512, 256, 256, 512, 4, 128


def gelu_tanh(v):
    return 0.5 * v * (1.0 + np.tanh(np.sqrt(2.0 / np.pi) * (v + 0.044715 * v**3)))


def setup_inputs():
    return {"base": bf(np.random.standard_normal((M, S))), "x": bf(np.random.standard_normal((K, N))), "w": bf(np.random.standard_normal((E, K, M)) / np.sqrt(K)), "b": f32(0.5 * np.random.standard_normal((M, 1))), "offs": striped(np.random.permutation(S))}


def reference(base, x, w, b, offs):
    idx = offs[:16].T.reshape(-1)
    z = f64(base).copy()
    for e in range(E):
        z[:, idx[e * Q : (e + 1) * Q]] += f64(w)[e].T @ f64(x)[:, e * Q : (e + 1) * Q]
    return gelu_tanh(z + f64(b))

@@ -1,0 +1,57 @@
+import concourse.mybir as mybir
+from concourse.masks import make_identity
+
+BF16, F32, U16 = mybir.dt.bfloat16, mybir.dt.float32, mybir.dt.uint16
+GELU = mybir.ActivationFunctionType.Gelu_apprx_tanh
+
+P = 128
+S = 512
+K = 256
+M = 256
+E = 4
+Q = 128
+KB = K // P
+MB = M // P
+QC = Q // 16
+
+FLOPS = 2 * K * M * E * Q
+
+
+def tile_scatter_matmul_kernel(tc, base, x, w, b, offs, out):
+    nc = tc.nc
+    with (
+        tc.tile_pool(name="held", bufs=1) as held,
+        tc.psum_pool(name="banks", bufs=1) as banks,
+    ):
+        offsets = held.tile([P, E * QC], U16, name="offsets")
+        nc.sync.dma_start(offsets[:], offs)
+
+        base_sb = held.tile([P, MB, S], BF16, name="base_sb")
+        nc.sync.dma_start(base_sb[:], base.rearrange("(a p) t -> p a t", p=P))
+        x_sb = held.tile([P, KB, E * Q], BF16, name="x_sb")
+        nc.scalar.dma_start(x_sb[:], x.rearrange("(c p) j -> p c j", p=P))
+        w_sb = held.tile([P, E * KB, M], BF16, name="w_sb")
+        nc.gpsimd.dma_start(w_sb[:], w.rearrange("e (c p) m -> p (e c) m", p=P))
+        bias = held.tile([P, MB], F32, name="bias")
+        nc.scalar.dma_start(bias[:], b.rearrange("(a p) o -> p (a o)", p=P))
+
+        ident = held.tile([P, P], BF16, name="ident")
+        make_identity(nc, ident[:])
+
+        windows = [banks.tile([P, S], F32, name="window%d" % a) for a in range(MB)]
+        for a in range(MB):
+            nc.tensor.matmul(windows[a][:], ident[:], base_sb[:, a, :], start=True, stop=False)
+
+        for a in range(MB):
+            for e in range(E):
+                for c in range(KB):
+                    nc.tensor.matmul(
+                        windows[a][:].indirect(offsets[:, e * QC : (e + 1) * QC]),
+                        w_sb[:, e * KB + c, a * P : (a + 1) * P],
+                        x_sb[:, c, e * Q : (e + 1) * Q],
+                        start=False,
+                        stop=(e == E - 1 and c == KB - 1),
+                    )
+            result = held.tile([P, S], F32, name="result%d" % a)
+            nc.scalar.activation(result[:], windows[a][:], GELU, bias=bias[:, a : a + 1])
+            nc.sync.dma_start(out[a * P : (a + 1) * P, :], result[:])

@@ -14,6 +14,8 @@ KB = K // P
 MB = M // P
 QC = Q // 16
 
+WARM_UP = 4
+
 FLOPS = 2 * K * M * E * Q
 
 
@@ -26,32 +28,48 @@ def tile_scatter_matmul_kernel(tc, base, x, w, b, offs, out):
         offsets = held.tile([P, E * QC], U16, name="offsets")
         nc.sync.dma_start(offsets[:], offs)
 
-        base_sb = held.tile([P, MB, S], BF16, name="base_sb")
-        nc.sync.dma_start(base_sb[:], base.rearrange("(a p) t -> p a t", p=P))
-        x_sb = held.tile([P, KB, E * Q], BF16, name="x_sb")
-        nc.scalar.dma_start(x_sb[:], x.rearrange("(c p) j -> p c j", p=P))
-        w_sb = held.tile([P, E * KB, M], BF16, name="w_sb")
-        nc.gpsimd.dma_start(w_sb[:], w.rearrange("e (c p) m -> p (e c) m", p=P))
+        queues = [nc.sync, nc.scalar]
+        base_sb = [held.tile([P, S], BF16, name="base_sb%d" % a) for a in range(MB)]
+        for a in range(MB):
+            queues[a % 2].dma_start(base_sb[a][:], base[a * P : (a + 1) * P, :])
+        x_sb = [held.tile([P, E * Q], BF16, name="x_sb%d" % c) for c in range(KB)]
+        for c in range(KB):
+            queues[c % 2].dma_start(x_sb[c][:], x[c * P : (c + 1) * P, :])
+        w_sb = [held.tile([P, KB, M], BF16, name="w_sb%d" % e) for e in range(E)]
+        for e in range(E):
+            queues[e % 2].dma_start(w_sb[e][:], w[e].rearrange("(c p) m -> p c m", p=P))
         bias = held.tile([P, MB], F32, name="bias")
         nc.scalar.dma_start(bias[:], b.rearrange("(a p) o -> p (a o)", p=P))
+
+        zeros = held.tile([P, S], BF16, name="zeros")
+        nc.vector.memset(zeros[:], 0.0)
+        idle_bank = banks.tile([P, S], F32, name="idle_bank")
+        for i in range(WARM_UP):
+            nc.tensor.matmul(idle_bank[:], zeros[:, 0:P], zeros[:], start=True, stop=True)
 
         ident = held.tile([P, P], BF16, name="ident")
         make_identity(nc, ident[:])
 
+        warm = held.tile([P, 1], F32, name="warm")
+        nc.vector.memset(warm[:], 0.0)
+        nc.scalar.activation(warm[:], warm[:], GELU)
+
         windows = [banks.tile([P, S], F32, name="window%d" % a) for a in range(MB)]
         for a in range(MB):
-            nc.tensor.matmul(windows[a][:], ident[:], base_sb[:, a, :], start=True, stop=False)
+            nc.tensor.matmul(windows[a][:], ident[:], base_sb[a][:], start=True, stop=False)
 
         for a in range(MB):
             for e in range(E):
                 for c in range(KB):
                     nc.tensor.matmul(
                         windows[a][:].indirect(offsets[:, e * QC : (e + 1) * QC]),
-                        w_sb[:, e * KB + c, a * P : (a + 1) * P],
-                        x_sb[:, c, e * Q : (e + 1) * Q],
+                        w_sb[e][:, c, a * P : (a + 1) * P],
+                        x_sb[c][:, e * Q : (e + 1) * Q],
                         start=False,
                         stop=(e == E - 1 and c == KB - 1),
                     )
             result = held.tile([P, S], F32, name="result%d" % a)
-            nc.scalar.activation(result[:], windows[a][:], GELU, bias=bias[:, a : a + 1])
-            nc.sync.dma_start(out[a * P : (a + 1) * P, :], result[:])
+            for h, queue in enumerate((nc.sync, nc.scalar)):
+                cols = slice(h * (S // 2), (h + 1) * (S // 2))
+                nc.scalar.activation(result[:, cols], windows[a][:, cols], GELU, bias=bias[:, a : a + 1])
+                queue.dma_start(out[a * P : (a + 1) * P, cols], result[:, cols])

@@ -14,8 +14,6 @@ KB = K // P
 MB = M // P
 QC = Q // 16
 
-WARM_UP = 4
-
 FLOPS = 2 * K * M * E * Q
 
 
@@ -41,12 +39,6 @@ def tile_scatter_matmul_kernel(tc, base, x, w, b, offs, out):
         bias = held.tile([P, MB], F32, name="bias")
         nc.scalar.dma_start(bias[:], b.rearrange("(a p) o -> p (a o)", p=P))
 
-        zeros = held.tile([P, S], BF16, name="zeros")
-        nc.vector.memset(zeros[:], 0.0)
-        idle_bank = banks.tile([P, S], F32, name="idle_bank")
-        for i in range(WARM_UP):
-            nc.tensor.matmul(idle_bank[:], zeros[:, 0:P], zeros[:], start=True, stop=True)
-
         ident = held.tile([P, P], BF16, name="ident")
         make_identity(nc, ident[:])
 
@@ -58,8 +50,8 @@ def tile_scatter_matmul_kernel(tc, base, x, w, b, offs, out):
         for a in range(MB):
             nc.tensor.matmul(windows[a][:], ident[:], base_sb[a][:], start=True, stop=False)
 
-        for a in range(MB):
-            for e in range(E):
+        for e in range(E):
+            for a in range(MB):
                 for c in range(KB):
                     nc.tensor.matmul(
                         windows[a][:].indirect(offsets[:, e * QC : (e + 1) * QC]),
@@ -68,6 +60,8 @@ def tile_scatter_matmul_kernel(tc, base, x, w, b, offs, out):
                         start=False,
                         stop=(e == E - 1 and c == KB - 1),
                     )
+
+        for a in range(MB):
             result = held.tile([P, S], F32, name="result%d" % a)
             for h, queue in enumerate((nc.sync, nc.scalar)):
                 cols = slice(h * (S // 2), (h + 1) * (S // 2))

@@ -13,6 +13,8 @@ Q = 128
 KB = K // P
 MB = M // P
 QC = Q // 16
+G = 2
+GQ = G * Q
 
 FLOPS = 2 * K * M * E * Q
 
@@ -26,18 +28,19 @@ def tile_scatter_matmul_kernel(tc, base, x, w, b, offs, out):
         offsets = held.tile([P, E * QC], U16, name="offsets")
         nc.sync.dma_start(offsets[:], offs)
 
-        queues = [nc.sync, nc.scalar]
-        base_sb = [held.tile([P, S], BF16, name="base_sb%d" % a) for a in range(MB)]
-        for a in range(MB):
-            queues[a % 2].dma_start(base_sb[a][:], base[a * P : (a + 1) * P, :])
-        x_sb = [held.tile([P, E * Q], BF16, name="x_sb%d" % c) for c in range(KB)]
-        for c in range(KB):
-            queues[c % 2].dma_start(x_sb[c][:], x[c * P : (c + 1) * P, :])
+        base_sb = held.tile([P, MB, S], BF16, name="base_sb")
+        x_sb = [held.tile([P, KB, GQ], BF16, name="x_sb%d" % g) for g in range(E // G)]
         w_sb = [held.tile([P, KB, M], BF16, name="w_sb%d" % e) for e in range(E)]
-        for e in range(E):
-            queues[e % 2].dma_start(w_sb[e][:], w[e].rearrange("(c p) m -> p c m", p=P))
         bias = held.tile([P, MB], F32, name="bias")
-        nc.scalar.dma_start(bias[:], b.rearrange("(a p) o -> p (a o)", p=P))
+
+        loads = [(base_sb, base.rearrange("(a p) t -> p a t", p=P))]
+        for g in range(E // G):
+            loads.append((x_sb[g], x[:, g * GQ : (g + 1) * GQ].rearrange("(c p) j -> p c j", p=P)))
+            for e in range(g * G, (g + 1) * G):
+                loads.append((w_sb[e], w[e].rearrange("(c p) m -> p c m", p=P)))
+        loads.append((bias, b.rearrange("(a p) o -> p (a o)", p=P)))
+        for i, (tile_sb, source) in enumerate(loads):
+            (nc.scalar, nc.sync)[i % 2].dma_start(tile_sb[:], source)
 
         ident = held.tile([P, P], BF16, name="ident")
         make_identity(nc, ident[:])
@@ -48,18 +51,19 @@ def tile_scatter_matmul_kernel(tc, base, x, w, b, offs, out):
 
         windows = [banks.tile([P, S], F32, name="window%d" % a) for a in range(MB)]
         for a in range(MB):
-            nc.tensor.matmul(windows[a][:], ident[:], base_sb[a][:], start=True, stop=False)
+            nc.tensor.matmul(windows[a][:], ident[:], base_sb[:, a, :], start=True, stop=False)
 
-        for e in range(E):
+        for g in range(E // G):
             for a in range(MB):
-                for c in range(KB):
-                    nc.tensor.matmul(
-                        windows[a][:].indirect(offsets[:, e * QC : (e + 1) * QC]),
-                        w_sb[e][:, c, a * P : (a + 1) * P],
-                        x_sb[c][:, e * Q : (e + 1) * Q],
-                        start=False,
-                        stop=(e == E - 1 and c == KB - 1),
-                    )
+                for e in range(g * G, (g + 1) * G):
+                    for c in range(KB):
+                        nc.tensor.matmul(
+                            windows[a][:].indirect(offsets[:, e * QC : (e + 1) * QC]),
+                            w_sb[e][:, c, a * P : (a + 1) * P],
+                            x_sb[g][:, c, (e - g * G) * Q : (e - g * G + 1) * Q],
+                            start=False,
+                            stop=(e == E - 1 and c == KB - 1),
+                        )
 
         for a in range(MB):
             result = held.tile([P, S], F32, name="result%d" % a)

@@ -14,7 +14,6 @@ KB = K // P
 MB = M // P
 QC = Q // 16
 G = 2
-GQ = G * Q
 
 FLOPS = 2 * K * M * E * Q
 
@@ -29,15 +28,14 @@ def tile_scatter_matmul_kernel(tc, base, x, w, b, offs, out):
         nc.sync.dma_start(offsets[:], offs)
 
         base_sb = held.tile([P, MB, S], BF16, name="base_sb")
-        x_sb = [held.tile([P, KB, GQ], BF16, name="x_sb%d" % g) for g in range(E // G)]
+        x_sb = held.tile([P, KB, E * Q], BF16, name="x_sb")
         w_sb = [held.tile([P, KB, M], BF16, name="w_sb%d" % e) for e in range(E)]
         bias = held.tile([P, MB], F32, name="bias")
 
         loads = [(base_sb, base.rearrange("(a p) t -> p a t", p=P))]
-        for g in range(E // G):
-            loads.append((x_sb[g], x[:, g * GQ : (g + 1) * GQ].rearrange("(c p) j -> p c j", p=P)))
-            for e in range(g * G, (g + 1) * G):
-                loads.append((w_sb[e], w[e].rearrange("(c p) m -> p c m", p=P)))
+        loads.append((x_sb, x.rearrange("(p c) j -> p c j", c=KB)))
+        for e in range(E):
+            loads.append((w_sb[e], w[e].rearrange("(p c) m -> p c m", c=KB)))
         loads.append((bias, b.rearrange("(a p) o -> p (a o)", p=P)))
         for i, (tile_sb, source) in enumerate(loads):
             (nc.scalar, nc.sync)[i % 2].dma_start(tile_sb[:], source)
@@ -60,7 +58,7 @@ def tile_scatter_matmul_kernel(tc, base, x, w, b, offs, out):
                         nc.tensor.matmul(
                             windows[a][:].indirect(offsets[:, e * QC : (e + 1) * QC]),
                             w_sb[e][:, c, a * P : (a + 1) * P],
-                            x_sb[g][:, c, (e - g * G) * Q : (e - g * G + 1) * Q],
+                            x_sb[:, c, e * Q : (e + 1) * Q],
                             start=False,
                             stop=(e == E - 1 and c == KB - 1),
                         )

@@ -14,6 +14,7 @@ KB = K // P
 MB = M // P
 QC = Q // 16
 G = 2
+WARM = 4
 
 FLOPS = 2 * K * M * E * Q
 
@@ -24,6 +25,9 @@ def tile_scatter_matmul_kernel(tc, base, x, w, b, offs, out):
         tc.tile_pool(name="held", bufs=1) as held,
         tc.psum_pool(name="banks", bufs=1) as banks,
     ):
+        zeros = held.tile([P, S], BF16, name="zeros")
+        nc.vector.memset(zeros[:], 0.0)
+
         offsets = held.tile([P, E * QC], U16, name="offsets")
         nc.sync.dma_start(offsets[:], offs)
 
@@ -46,6 +50,10 @@ def tile_scatter_matmul_kernel(tc, base, x, w, b, offs, out):
         warm = held.tile([P, 1], F32, name="warm")
         nc.vector.memset(warm[:], 0.0)
         nc.scalar.activation(warm[:], warm[:], GELU)
+
+        spare = banks.tile([P, S], F32, name="spare")
+        for i in range(WARM):
+            nc.tensor.matmul(spare[:], zeros[:, 0:P], zeros[:], start=True, stop=True)
 
         windows = [banks.tile([P, S], F32, name="window%d" % a) for a in range(MB)]
         for a in range(MB):

@@ -13,7 +13,6 @@ Q = 128
 KB = K // P
 MB = M // P
 QC = Q // 16
-G = 2
 WARM = 4
 
 FLOPS = 2 * K * M * E * Q
@@ -59,17 +58,16 @@ def tile_scatter_matmul_kernel(tc, base, x, w, b, offs, out):
         for a in range(MB):
             nc.tensor.matmul(windows[a][:], ident[:], base_sb[:, a, :], start=True, stop=False)
 
-        for g in range(E // G):
-            for a in range(MB):
-                for e in range(g * G, (g + 1) * G):
-                    for c in range(KB):
-                        nc.tensor.matmul(
-                            windows[a][:].indirect(offsets[:, e * QC : (e + 1) * QC]),
-                            w_sb[e][:, c, a * P : (a + 1) * P],
-                            x_sb[:, c, e * Q : (e + 1) * Q],
-                            start=False,
-                            stop=(e == E - 1 and c == KB - 1),
-                        )
+        for a in range(MB):
+            for e in range(E):
+                for c in range(KB):
+                    nc.tensor.matmul(
+                        windows[a][:].indirect(offsets[:, e * QC : (e + 1) * QC]),
+                        w_sb[e][:, c, a * P : (a + 1) * P],
+                        x_sb[:, c, e * Q : (e + 1) * Q],
+                        start=False,
+                        stop=(e == E - 1 and c == KB - 1),
+                    )
 
         for a in range(MB):
             result = held.tile([P, S], F32, name="result%d" % a)

@@ -13,7 +13,7 @@ Q = 128
 KB = K // P
 MB = M // P
 QC = Q // 16
-WARM = 4
+WARM = 3
 
 FLOPS = 2 * K * M * E * Q
 

@@ -13,6 +13,7 @@ Q = 128
 KB = K // P
 MB = M // P
 QC = Q // 16
+G = 2
 WARM = 3
 
 FLOPS = 2 * K * M * E * Q
@@ -24,27 +25,30 @@ def tile_scatter_matmul_kernel(tc, base, x, w, b, offs, out):
         tc.tile_pool(name="held", bufs=1) as held,
         tc.psum_pool(name="banks", bufs=1) as banks,
     ):
+        ident = held.tile([P, P], BF16, name="ident")
+        nc.vector.memset(ident[:], 0.0)
+        make_identity(nc, ident[:], nomemset=True)
+
         zeros = held.tile([P, S], BF16, name="zeros")
         nc.vector.memset(zeros[:], 0.0)
 
         offsets = held.tile([P, E * QC], U16, name="offsets")
-        nc.sync.dma_start(offsets[:], offs)
-
         base_sb = held.tile([P, MB, S], BF16, name="base_sb")
-        x_sb = held.tile([P, KB, E * Q], BF16, name="x_sb")
-        w_sb = [held.tile([P, KB, M], BF16, name="w_sb%d" % e) for e in range(E)]
+        x_sb = [held.tile([P, E * Q], BF16, name="x_sb%d" % c) for c in range(KB)]
+        x_blocks = x.rearrange("(p c) j -> p c j", c=KB)
+        w_first = [held.tile([P, KB, M], BF16, name="w_first%d" % e) for e in range(G)]
+        w_second = held.tile([P, E - G, KB, M], BF16, name="w_second")
+        w_sb = [w_first[e][:] for e in range(G)] + [w_second[:, e - G] for e in range(G, E)]
         bias = held.tile([P, MB], F32, name="bias")
 
-        loads = [(base_sb, base.rearrange("(a p) t -> p a t", p=P))]
-        loads.append((x_sb, x.rearrange("(p c) j -> p c j", c=KB)))
-        for e in range(E):
-            loads.append((w_sb[e], w[e].rearrange("(p c) m -> p c m", c=KB)))
-        loads.append((bias, b.rearrange("(a p) o -> p (a o)", p=P)))
-        for i, (tile_sb, source) in enumerate(loads):
-            (nc.scalar, nc.sync)[i % 2].dma_start(tile_sb[:], source)
-
-        ident = held.tile([P, P], BF16, name="ident")
-        make_identity(nc, ident[:])
+        nc.sync.dma_start(base_sb[:], base.rearrange("(a p) t -> p a t", p=P))
+        nc.sync.dma_start(offsets[:], offs)
+        nc.sync.dma_start(x_sb[0][:], x_blocks[:, 0, :])
+        nc.sync.dma_start(w_first[0][:], w[0].rearrange("(p c) m -> p c m", c=KB))
+        nc.sync.dma_start(x_sb[1][:], x_blocks[:, 1, :])
+        nc.sync.dma_start(w_first[1][:], w[1].rearrange("(p c) m -> p c m", c=KB))
+        nc.sync.dma_start(w_second[:], w[G:E].rearrange("e (p c) m -> p e c m", c=KB))
+        nc.sync.dma_start(bias[:], b.rearrange("(a p) o -> p (a o)", p=P))
 
         warm = held.tile([P, 1], F32, name="warm")
         nc.vector.memset(warm[:], 0.0)
@@ -58,16 +62,16 @@ def tile_scatter_matmul_kernel(tc, base, x, w, b, offs, out):
         for a in range(MB):
             nc.tensor.matmul(windows[a][:], ident[:], base_sb[:, a, :], start=True, stop=False)
 
-        for a in range(MB):
-            for e in range(E):
-                for c in range(KB):
-                    nc.tensor.matmul(
-                        windows[a][:].indirect(offsets[:, e * QC : (e + 1) * QC]),
-                        w_sb[e][:, c, a * P : (a + 1) * P],
-                        x_sb[:, c, e * Q : (e + 1) * Q],
-                        start=False,
-                        stop=(e == E - 1 and c == KB - 1),
-                    )
+        order = [(e, c, a) for e in range(G) for c in range(KB) for a in range(MB)]
+        order += [(e, c, a) for a in range(MB) for e in range(G, E) for c in range(KB)]
+        for e, c, a in order:
+            nc.tensor.matmul(
+                windows[a][:].indirect(offsets[:, e * QC : (e + 1) * QC]),
+                w_sb[e][:, c, a * P : (a + 1) * P],
+                x_sb[c][:, e * Q : (e + 1) * Q],
+                start=False,
+                stop=(e == E - 1 and c == KB - 1),
+            )
 
         for a in range(MB):
             result = held.tile([P, S], F32, name="result%d" % a)

@@ -14,6 +14,7 @@ KB = K // P
 MB = M // P
 QC = Q // 16
 G = 2
+HEAD = G * Q
 WARM = 3
 
 FLOPS = 2 * K * M * E * Q
@@ -34,8 +35,9 @@ def tile_scatter_matmul_kernel(tc, base, x, w, b, offs, out):
 
         offsets = held.tile([P, E * QC], U16, name="offsets")
         base_sb = held.tile([P, MB, S], BF16, name="base_sb")
-        x_sb = [held.tile([P, E * Q], BF16, name="x_sb%d" % c) for c in range(KB)]
-        x_blocks = x.rearrange("(p c) j -> p c j", c=KB)
+        x_runs = x.rearrange("(p c) j -> p (c j)", c=KB)
+        x_head = held.tile([P, HEAD], BF16, name="x_head")
+        x_rest = held.tile([P, KB * E * Q - HEAD], BF16, name="x_rest")
         w_first = [held.tile([P, KB, M], BF16, name="w_first%d" % e) for e in range(G)]
         w_second = held.tile([P, E - G, KB, M], BF16, name="w_second")
         w_sb = [w_first[e][:] for e in range(G)] + [w_second[:, e - G] for e in range(G, E)]
@@ -43,10 +45,10 @@ def tile_scatter_matmul_kernel(tc, base, x, w, b, offs, out):
 
         nc.sync.dma_start(base_sb[:], base.rearrange("(a p) t -> p a t", p=P))
         nc.sync.dma_start(offsets[:], offs)
-        nc.sync.dma_start(x_sb[0][:], x_blocks[:, 0, :])
+        nc.sync.dma_start(x_head[:], x_runs[:, 0:HEAD])
         nc.sync.dma_start(w_first[0][:], w[0].rearrange("(p c) m -> p c m", c=KB))
-        nc.sync.dma_start(x_sb[1][:], x_blocks[:, 1, :])
         nc.sync.dma_start(w_first[1][:], w[1].rearrange("(p c) m -> p c m", c=KB))
+        nc.sync.dma_start(x_rest[:], x_runs[:, HEAD : KB * E * Q])
         nc.sync.dma_start(w_second[:], w[G:E].rearrange("e (p c) m -> p e c m", c=KB))
         nc.sync.dma_start(bias[:], b.rearrange("(a p) o -> p (a o)", p=P))
 
@@ -62,13 +64,19 @@ def tile_scatter_matmul_kernel(tc, base, x, w, b, offs, out):
         for a in range(MB):
             nc.tensor.matmul(windows[a][:], ident[:], base_sb[:, a, :], start=True, stop=False)
 
-        order = [(e, c, a) for e in range(G) for c in range(KB) for a in range(MB)]
+        def x_columns(e, c):
+            place = c * E * Q + e * Q
+            if place < HEAD:
+                return x_head[:, place : place + Q]
+            return x_rest[:, place - HEAD : place - HEAD + Q]
+
+        order = [(e, c, a) for c in range(KB) for e in range(G) for a in range(MB)]
         order += [(e, c, a) for a in range(MB) for e in range(G, E) for c in range(KB)]
         for e, c, a in order:
             nc.tensor.matmul(
                 windows[a][:].indirect(offsets[:, e * QC : (e + 1) * QC]),
                 w_sb[e][:, c, a * P : (a + 1) * P],
-                x_sb[c][:, e * Q : (e + 1) * Q],
+                x_columns(e, c),
                 start=False,
                 stop=(e == E - 1 and c == KB - 1),
             )

@@ -15,6 +15,7 @@ MB = M // P
 QC = Q // 16
 G = 2
 HEAD = G * Q
+LINE = 256
 WARM = 3
 
 FLOPS = 2 * K * M * E * Q
@@ -34,12 +35,12 @@ def tile_scatter_matmul_kernel(tc, base, x, w, b, offs, out):
         nc.vector.memset(zeros[:], 0.0)
 
         offsets = held.tile([P, E * QC], U16, name="offsets")
-        base_sb = held.tile([P, MB, S], BF16, name="base_sb")
+        base_sb = held.tile([P, MB, S], BF16, name="base_sb", align_bytes=LINE)
         x_runs = x.rearrange("(p c) j -> p (c j)", c=KB)
-        x_head = held.tile([P, HEAD], BF16, name="x_head")
-        x_rest = held.tile([P, KB * E * Q - HEAD], BF16, name="x_rest")
-        w_first = [held.tile([P, KB, M], BF16, name="w_first%d" % e) for e in range(G)]
-        w_second = held.tile([P, E - G, KB, M], BF16, name="w_second")
+        x_head = held.tile([P, HEAD], BF16, name="x_head", align_bytes=LINE)
+        x_rest = held.tile([P, KB * E * Q - HEAD], BF16, name="x_rest", align_bytes=LINE)
+        w_first = [held.tile([P, KB, M], BF16, name="w_first%d" % e, align_bytes=LINE) for e in range(G)]
+        w_second = held.tile([P, E - G, KB, M], BF16, name="w_second", align_bytes=LINE)
         w_sb = [w_first[e][:] for e in range(G)] + [w_second[:, e - G] for e in range(G, E)]
         bias = held.tile([P, MB], F32, name="bias")
 
@@ -82,7 +83,7 @@ def tile_scatter_matmul_kernel(tc, base, x, w, b, offs, out):
             )
 
         for a in range(MB):
-            result = held.tile([P, S], F32, name="result%d" % a)
+            result = held.tile([P, S], F32, name="result%d" % a, align_bytes=LINE)
             for h, queue in enumerate((nc.sync, nc.scalar)):
                 cols = slice(h * (S // 2), (h + 1) * (S // 2))
                 nc.scalar.activation(result[:, cols], windows[a][:, cols], GELU, bias=bias[:, a : a + 1])

@@ -16,6 +16,7 @@ QC = Q // 16
 G = 2
 HEAD = G * Q
 LINE = 256
+PAD = 8
 WARM = 3
 
 FLOPS = 2 * K * M * E * Q
@@ -42,7 +43,7 @@ def tile_scatter_matmul_kernel(tc, base, x, w, b, offs, out):
         w_first = [held.tile([P, KB, M], BF16, name="w_first%d" % e, align_bytes=LINE) for e in range(G)]
         w_second = held.tile([P, E - G, KB, M], BF16, name="w_second", align_bytes=LINE)
         w_sb = [w_first[e][:] for e in range(G)] + [w_second[:, e - G] for e in range(G, E)]
-        bias = held.tile([P, MB], F32, name="bias")
+        bias = held.tile([P, MB, PAD], F32, name="bias")
 
         nc.sync.dma_start(base_sb[:], base.rearrange("(a p) t -> p a t", p=P))
         nc.sync.dma_start(offsets[:], offs)
@@ -51,7 +52,7 @@ def tile_scatter_matmul_kernel(tc, base, x, w, b, offs, out):
         nc.sync.dma_start(w_first[1][:], w[1].rearrange("(p c) m -> p c m", c=KB))
         nc.sync.dma_start(x_rest[:], x_runs[:, HEAD : KB * E * Q])
         nc.sync.dma_start(w_second[:], w[G:E].rearrange("e (p c) m -> p e c m", c=KB))
-        nc.sync.dma_start(bias[:], b.rearrange("(a p) o -> p (a o)", p=P))
+        nc.sync.dma_start(bias[:, :, 0:1], b.rearrange("(a p) o -> p a o", p=P))
 
         warm = held.tile([P, 1], F32, name="warm")
         nc.vector.memset(warm[:], 0.0)
@@ -86,5 +87,5 @@ def tile_scatter_matmul_kernel(tc, base, x, w, b, offs, out):
             result = held.tile([P, S], F32, name="result%d" % a, align_bytes=LINE)
             for h, queue in enumerate((nc.sync, nc.scalar)):
                 cols = slice(h * (S // 2), (h + 1) * (S // 2))
-                nc.scalar.activation(result[:, cols], windows[a][:, cols], GELU, bias=bias[:, a : a + 1])
+                nc.scalar.activation(result[:, cols], windows[a][:, cols], GELU, bias=bias[:, a, 0:1])
                 queue.dma_start(out[a * P : (a + 1) * P, cols], result[:, cols])

@@ -85,7 +85,8 @@ def tile_scatter_matmul_kernel(tc, base, x, w, b, offs, out):
 
         for a in range(MB):
             result = held.tile([P, S], F32, name="result%d" % a, align_bytes=LINE)
-            for h, queue in enumerate((nc.sync, nc.scalar)):
+            for h in range(2):
+                queue = nc.scalar if (a == MB - 1 and h == 1) else nc.sync
                 cols = slice(h * (S // 2), (h + 1) * (S // 2))
                 nc.scalar.activation(result[:, cols], windows[a][:, cols], GELU, bias=bias[:, a, 0:1])
                 queue.dma_start(out[a * P : (a + 1) * P, cols], result[:, cols])

@@ -86,7 +86,6 @@ def tile_scatter_matmul_kernel(tc, base, x, w, b, offs, out):
         for a in range(MB):
             result = held.tile([P, S], F32, name="result%d" % a, align_bytes=LINE)
             for h in range(2):
-                queue = nc.scalar if (a == MB - 1 and h == 1) else nc.sync
                 cols = slice(h * (S // 2), (h + 1) * (S // 2))
                 nc.scalar.activation(result[:, cols], windows[a][:, cols], GELU, bias=bias[:, a, 0:1])
-                queue.dma_start(out[a * P : (a + 1) * P, cols], result[:, cols])
+                nc.sync.dma_start(out[a * P : (a + 1) * P, cols], result[:, cols])

import concourse.mybir as mybir
from concourse.masks import make_identity

BF16, F32, U16 = mybir.dt.bfloat16, mybir.dt.float32, mybir.dt.uint16
GELU = mybir.ActivationFunctionType.Gelu_apprx_tanh

P = 128
S = 512
K = 256
M = 256
E = 4
Q = 128
KB = K // P
MB = M // P
QC = Q // 16
G = 2
HEAD = G * Q
LINE = 256
PAD = 8
WARM = 3

FLOPS = 2 * K * M * E * Q


def tile_scatter_matmul_kernel(tc, base, x, w, b, offs, out):
    nc = tc.nc
    with (
        tc.tile_pool(name="held", bufs=1) as held,
        tc.psum_pool(name="banks", bufs=1) as banks,
    ):
        ident = held.tile([P, P], BF16, name="ident")
        nc.vector.memset(ident[:], 0.0)
        make_identity(nc, ident[:], nomemset=True)

        zeros = held.tile([P, S], BF16, name="zeros")
        nc.vector.memset(zeros[:], 0.0)

        offsets = held.tile([P, E * QC], U16, name="offsets")
        base_sb = held.tile([P, MB, S], BF16, name="base_sb", align_bytes=LINE)
        x_runs = x.rearrange("(p c) j -> p (c j)", c=KB)
        x_head = held.tile([P, HEAD], BF16, name="x_head", align_bytes=LINE)
        x_rest = held.tile([P, KB * E * Q - HEAD], BF16, name="x_rest", align_bytes=LINE)
        w_first = [held.tile([P, KB, M], BF16, name="w_first%d" % e, align_bytes=LINE) for e in range(G)]
        w_second = held.tile([P, E - G, KB, M], BF16, name="w_second", align_bytes=LINE)
        w_sb = [w_first[e][:] for e in range(G)] + [w_second[:, e - G] for e in range(G, E)]
        bias = held.tile([P, MB, PAD], F32, name="bias")

        nc.sync.dma_start(base_sb[:], base.rearrange("(a p) t -> p a t", p=P))
        nc.sync.dma_start(offsets[:], offs)
        nc.sync.dma_start(x_head[:], x_runs[:, 0:HEAD])
        nc.sync.dma_start(w_first[0][:], w[0].rearrange("(p c) m -> p c m", c=KB))
        nc.sync.dma_start(w_first[1][:], w[1].rearrange("(p c) m -> p c m", c=KB))
        nc.sync.dma_start(x_rest[:], x_runs[:, HEAD : KB * E * Q])
        nc.sync.dma_start(w_second[:], w[G:E].rearrange("e (p c) m -> p e c m", c=KB))
        nc.sync.dma_start(bias[:, :, 0:1], b.rearrange("(a p) o -> p a o", p=P))

        warm = held.tile([P, 1], F32, name="warm")
        nc.vector.memset(warm[:], 0.0)
        nc.scalar.activation(warm[:], warm[:], GELU)

        spare = banks.tile([P, S], F32, name="spare")
        for i in range(WARM):
            nc.tensor.matmul(spare[:], zeros[:, 0:P], zeros[:], start=True, stop=True)

        windows = [banks.tile([P, S], F32, name="window%d" % a) for a in range(MB)]
        for a in range(MB):
            nc.tensor.matmul(windows[a][:], ident[:], base_sb[:, a, :], start=True, stop=False)

        def x_columns(e, c):
            place = c * E * Q + e * Q
            if place < HEAD:
                return x_head[:, place : place + Q]
            return x_rest[:, place - HEAD : place - HEAD + Q]

        order = [(e, c, a) for c in range(KB) for e in range(G) for a in range(MB)]
        order += [(e, c, a) for a in range(MB) for e in range(G, E) for c in range(KB)]
        for e, c, a in order:
            nc.tensor.matmul(
                windows[a][:].indirect(offsets[:, e * QC : (e + 1) * QC]),
                w_sb[e][:, c, a * P : (a + 1) * P],
                x_columns(e, c),
                start=False,
                stop=(e == E - 1 and c == KB - 1),
            )

        for a in range(MB):
            result = held.tile([P, S], F32, name="result%d" % a, align_bytes=LINE)
            for h in range(2):
                cols = slice(h * (S // 2), (h + 1) * (S // 2))
                nc.scalar.activation(result[:, cols], windows[a][:, cols], GELU, bias=bias[:, a, 0:1])
                nc.sync.dma_start(out[a * P : (a + 1) * P, cols], result[:, cols])
